import numpy as np
import ml_dtypes


def mxq(x, axis, fmt="e4m3"):
    dtype, down = {"e4m3": (ml_dtypes.float8_e4m3fn, 7), "e5m2": (ml_dtypes.float8_e5m2, 14)}[fmt]
    v = np.moveaxis(np.asarray(x, np.float32).astype(ml_dtypes.bfloat16).astype(np.float64), axis, -1)
    blocks = v.reshape(v.shape[:-1] + (-1, 32))
    amax = np.abs(blocks).max(-1, keepdims=True)
    byte = np.maximum(np.where(amax > 0, np.frexp(amax)[1] - 1 + 127, 0) - down, 1)
    scale = np.exp2(byte - 127.0)
    codes = (blocks / scale).astype(np.float32).astype(dtype).astype(np.float64)
    return np.moveaxis((codes * scale).reshape(v.shape), -1, axis)


WIDE = False


def mx_kscale(k):
    if not WIDE:
        return np.ones(k)
    levels = np.array([10, -10, 5, -5, 0])
    if k % 512:
        return np.exp2(np.random.permutation(np.resize(levels, k // 32))).repeat(32)
    a = np.empty((k // 512, 16))
    for p in range(k // 512):
        a[p, :8] = np.random.permutation(np.resize(levels, 8))
        for g in range(8):
            far = levels[np.abs(levels - a[p, g]) >= 10]
            a[p, g + 8] = far[np.random.randint(len(far))]
    return np.exp2(a.ravel()).repeat(32)


def f64(x):
    return np.asarray(x).astype(np.float64)


def striped(idx):
    return np.tile(idx.reshape(-1, 16).T, (8, 1)).astype(np.uint16)


def unstriped(offs):
    return offs[:16].T.reshape(-1).astype(np.int64)


def gelu(v):
    return 0.5 * v * (1.0 + np.tanh(np.sqrt(2.0 / np.pi) * (v + 0.044715 * v**3)))


K, T, S, H, N = 512, 2048, 1024, 1024, 512


def setup_inputs():
    n = np.random.standard_normal
    s = mx_kscale(K)[:, None]
    u = mx_kscale(H)
    return {
        "xT": (n((K, S)) * s).astype(np.float32),
        "w1": (n((K, H)) / np.sqrt(K) / s * u).astype(np.float32),
        "w2": (n((H, N)) / np.sqrt(H) / u[:, None]).astype(np.float32),
        "gate": np.tile(np.random.uniform(0.2, 1.0, S), (N, 1)).astype(np.float32),
        "offs": striped(np.sort(np.random.permutation(T)[:S])),
    }


def reference(xT, w1, w2, gate, offs):
    idx = unstriped(offs)
    xq = mxq(f64(xT), 0, "e4m3")
    h = gelu(mxq(f64(w1), 0, "e4m3").T @ xq)
    y = mxq(f64(w2), 0, "e4m3").T @ mxq(h, 0, "e4m3")
    out = np.zeros((N, T))
    out[:, idx] = f64(gate) * y
    return out

@@ -1,0 +1,189 @@
+from contextlib import ExitStack
+
+import concourse.mybir as mybir
+
+K, T, S, H, N = 512, 2048, 1024, 1024, 512
+FLOPS = 2 * S * (K * H + H * N)
+BYTES = 4 * (K * S + K * H + H * N + S + N * T) + 2 * 128 * S // 16
+
+F32 = mybir.dt.float32
+BF16 = mybir.dt.bfloat16
+U32 = mybir.dt.uint32
+U16 = mybir.dt.uint16
+U8 = mybir.dt.uint8
+FP8X4 = mybir.dt.float8_e4m3fn_x4
+GELU = mybir.ActivationFunctionType.Gelu_apprx_tanh
+MULT = mybir.AluOpType.mult
+
+P = 128
+HALF = 512
+BLK = 128
+
+
+def tile_picked_place_mlp_gelu_srt_l_kernel(tc, xT, w1, w2, gate, offs, out):
+    nc = tc.nc
+    with ExitStack() as ctx:
+        keep = ctx.enter_context(tc.tile_pool(name="keep", bufs=1))
+        psum_h = ctx.enter_context(tc.psum_pool(name="psum_h", bufs=4))
+        psum_y = ctx.enter_context(tc.psum_pool(name="psum_y", bufs=4))
+
+        offsets = keep.tile([P, S // 16], U16, name="offsets")
+        gate_sb = keep.tile([P, S], F32, name="gate_sb")
+        warm = keep.tile([P, 8], F32, name="warm")
+        nc.vector.memset(warm[:], 0.0)
+        nc.scalar.activation(warm[:], warm[:], GELU)
+
+        x_rows = xT.rearrange("(p j) s -> p j s", j=4)
+        w1_rows = w1.rearrange("(p j) h -> p j h", j=4)
+
+        def load(name, src, width):
+            raw = keep.tile([P, 4, width], F32, name=name)
+            nc.sync.dma_start(out=raw[:], in_=src)
+            return raw
+
+        x_edges = [(0, 256), (256, 512), (512, 1024)]
+        x_raw = {}
+        w1_raw = {}
+        w2_raw = {}
+        x_raw[0] = load("x_raw0", x_rows[:, :, 0:256], 256)
+        w1_raw[0] = load("w1_raw0", w1_rows[:, :, 0:HALF], HALF)
+        x_raw[1] = load("x_raw1", x_rows[:, :, 256:512], 256)
+        w1_raw[1] = load("w1_raw1", w1_rows[:, :, HALF:H], HALF)
+        x_raw[2] = load("x_raw2", x_rows[:, :, 512:1024], 512)
+        nc.sync.dma_start(offsets[:], offs)
+        nc.sync.dma_start(out=gate_sb[:], in_=gate[0:P, :])
+        for c in range(2):
+            rows = w2[c * HALF : (c + 1) * HALF, :].rearrange("(p j) m -> p j m", j=4)
+            w2_raw[c] = load(f"w2_raw{c}", rows, N)
+
+        windows = []
+        for m in range(4):
+            window = keep.tile([P, T], F32, name=f"window{m}")
+            if m < 3:
+                nc.vector.memset(window[:], 0.0)
+            else:
+                nc.gpsimd.memset(window[:], 0.0)
+            windows.append(window)
+
+        def cast(grouped, raw, share):
+            n = grouped.shape[1]
+            cut = int(n * share) // 4 * 4
+            if cut > 0:
+                nc.vector.tensor_copy(out=grouped[:, 0:cut], in_=raw[:, 0:cut])
+            if cut < n:
+                nc.scalar.copy(out=grouped[:, cut:n], in_=raw[:, cut:n])
+
+        def quantize(codes, scales, grouped):
+            nc.vector.quantize_mx(out=codes.bitcast(FP8X4), scales=scales, in_=grouped)
+
+        x_codes = keep.tile([P, S], U32, name="x_codes", align_bytes=64)
+        x_scales = keep.tile([P, S], U8, name="x_scales", align_bytes=64)
+        w1_codes = keep.tile([P, 2, HALF], U32, name="w1_codes", align_bytes=64)
+        w1_scales = keep.tile([P, 2, HALF], U8, name="w1_scales", align_bytes=64)
+        w2_codes = keep.tile([P, 2, N], U32, name="w2_codes", align_bytes=64)
+        w2_scales = keep.tile([P, 2, N], U8, name="w2_scales", align_bytes=64)
+        h_codes = keep.tile([P, 2, S], U32, name="h_codes", align_bytes=64)
+        h_scales = keep.tile([P, 2, S], U8, name="h_scales", align_bytes=64)
+
+        def do_x(i, share):
+            a, b = x_edges[i]
+            n = b - a
+            g = keep.tile([P, 4 * n], BF16, name=f"x_grouped{i}", align_bytes=64)
+            cast(
+                g[:].rearrange("p (c i t) -> p c t i", i=4, t=4),
+                x_raw[i][:].rearrange("p t (c i) -> p c t i", i=4),
+                share,
+            )
+            quantize(x_codes[:, a:b], x_scales[:, a:b], g[:])
+
+        def do_w1(c, share):
+            g = keep.tile([P, 4 * HALF], BF16, name=f"w1_grouped{c}", align_bytes=64)
+            cast(
+                g[:].rearrange("p (t m j) -> p m j t", t=4, j=4),
+                w1_raw[c][:].rearrange("p j (m t) -> p m j t", t=4),
+                share,
+            )
+            quantize(w1_codes[:, c, :], w1_scales[:, c, :], g[:])
+
+        def do_w2(c, share):
+            g = keep.tile([P, 4 * N], BF16, name=f"w2_grouped{c}", align_bytes=64)
+            cast(
+                g[:].rearrange("p (c i t) -> p c t i", i=4, t=4),
+                w2_raw[c][:].rearrange("p t (c i) -> p c t i", i=4),
+                share,
+            )
+            quantize(w2_codes[:, c, :], w2_scales[:, c, :], g[:])
+
+        h_grouped = {}
+        for c in range(2):
+            for half in range(2):
+                h_grouped[c, half] = keep.tile([P, HALF, 4], BF16, name=f"h_grouped{c}{half}", align_bytes=64)
+
+        def layer1(c, b):
+            bank = psum_h.tile([P, 4, BLK], F32, name="bank")
+            cols = slice(b * BLK, (b + 1) * BLK)
+            for t in range(4):
+                nc.tensor.matmul_mx(
+                    out=bank[:, t, :],
+                    lhsT=w1_codes[:, c, t * P : (t + 1) * P].bitcast(FP8X4),
+                    lhsT_scale=w1_scales[:, c, t * P : (t + 1) * P],
+                    rhs=x_codes[:, cols].bitcast(FP8X4),
+                    rhs_scale=x_scales[:, cols],
+                    start=True,
+                    stop=True,
+                )
+            half, q = divmod(b, 4)
+            nc.scalar.activation(
+                h_grouped[c, half][:, q * BLK : (q + 1) * BLK, :],
+                bank[:].rearrange("p t n -> p n t"),
+                GELU,
+            )
+
+        def quant_h(c, half):
+            cols = slice(half * HALF, (half + 1) * HALF)
+            quantize(h_codes[:, c, cols], h_scales[:, c, cols], h_grouped[c, half][:].rearrange("p n t -> p (n t)"))
+
+        def layer2(half, m):
+            bank = psum_y.tile([P, HALF], F32, name="ybank")
+            cols = slice(half * HALF, (half + 1) * HALF)
+            for c in range(2):
+                nc.tensor.matmul_mx(
+                    out=bank[:],
+                    lhsT=w2_codes[:, c, m * P : (m + 1) * P].bitcast(FP8X4),
+                    lhsT_scale=w2_scales[:, c, m * P : (m + 1) * P],
+                    rhs=h_codes[:, c, cols].bitcast(FP8X4),
+                    rhs_scale=h_scales[:, c, cols],
+                    start=(c == 0),
+                    stop=(c == 1),
+                )
+            y = keep.tile([P, HALF], F32, name=f"y{half}{m}")
+            nc.scalar.copy(out=y[:], in_=bank[:])
+            nc.vector.tensor_tensor(
+                windows[m][:].indirect(offsets[:, half * 32 : (half + 1) * 32]), y[:], gate_sb[:, cols], MULT
+            )
+            if half == 1:
+                nc.sync.dma_start(out=out[m * P : (m + 1) * P, :], in_=windows[m][:])
+
+        do_x(0, 1.0)
+        do_w1(0, 0.6)
+        do_x(1, 1.0)
+        for b in range(0, 4):
+            layer1(0, b)
+        do_w1(1, 0.6)
+        quant_h(0, 0)
+        for b in range(0, 4):
+            layer1(1, b)
+        do_x(2, 1.0)
+        for b in range(4, 8):
+            layer1(0, b)
+        quant_h(1, 0)
+        do_w2(0, 1.0)
+        for b in range(4, 8):
+            layer1(1, b)
+        do_w2(1, 1.0)
+        quant_h(0, 1)
+        quant_h(1, 1)
+        for m in range(4):
+            layer2(0, m)
+        for m in range(4):
+            layer2(1, m)

@@ -16,8 +16,6 @@ GELU = mybir.ActivationFunctionType.Gelu_apprx_tanh
 MULT = mybir.AluOpType.mult
 
 P = 128
-HALF = 512
-BLK = 128
 
 
 def tile_picked_place_mlp_gelu_srt_l_kernel(tc, xT, w1, w2, gate, offs, out):
@@ -41,33 +39,43 @@ def tile_picked_place_mlp_gelu_srt_l_kernel(tc, xT, w1, w2, gate, offs, out):
             nc.sync.dma_start(out=raw[:], in_=src)
             return raw
 
-        x_edges = [(0, 256), (256, 512), (512, 1024)]
-        x_raw = {}
-        w1_raw = {}
-        w2_raw = {}
+        def load_w2(c, mh):
+            rows = w2[512 * c : 512 * (c + 1), 256 * mh : 256 * (mh + 1)].rearrange("(p j) m -> p j m", j=4)
+            return load(f"w2_raw{c}{mh}", rows, 256)
+
+        tokens = [(0, 256), (256, 512), (512, 1024)]
+        x_raw, w1_raw, w2_raw = {}, {}, {}
         x_raw[0] = load("x_raw0", x_rows[:, :, 0:256], 256)
-        w1_raw[0] = load("w1_raw0", w1_rows[:, :, 0:HALF], HALF)
+        w1_raw[0] = load("w1_raw0", w1_rows[:, :, 0:512], 512)
+        w1_raw[1] = load("w1_raw1", w1_rows[:, :, 512:1024], 512)
+        w2_raw[0, 0] = load_w2(0, 0)
+        w2_raw[1, 0] = load_w2(1, 0)
         x_raw[1] = load("x_raw1", x_rows[:, :, 256:512], 256)
-        w1_raw[1] = load("w1_raw1", w1_rows[:, :, HALF:H], HALF)
-        x_raw[2] = load("x_raw2", x_rows[:, :, 512:1024], 512)
         nc.sync.dma_start(offsets[:], offs)
         nc.sync.dma_start(out=gate_sb[:], in_=gate[0:P, :])
-        for c in range(2):
-            rows = w2[c * HALF : (c + 1) * HALF, :].rearrange("(p j) m -> p j m", j=4)
-            w2_raw[c] = load(f"w2_raw{c}", rows, N)
+        x_raw[2] = load("x_raw2", x_rows[:, :, 512:1024], 512)
+        w2_raw[0, 1] = load_w2(0, 1)
+        w2_raw[1, 1] = load_w2(1, 1)
 
         windows = []
         for m in range(4):
             window = keep.tile([P, T], F32, name=f"window{m}")
-            if m < 3:
-                nc.vector.memset(window[:], 0.0)
-            else:
-                nc.gpsimd.memset(window[:], 0.0)
             windows.append(window)
+        nc.vector.memset(windows[0][:], 0.0)
+        nc.vector.memset(windows[1][:], 0.0)
+
+        x_codes = keep.tile([P, S], U32, name="x_codes", align_bytes=64)
+        x_scales = keep.tile([P, S], U8, name="x_scales", align_bytes=64)
+        w1_codes = keep.tile([P, 2, 512], U32, name="w1_codes", align_bytes=64)
+        w1_scales = keep.tile([P, 2, 512], U8, name="w1_scales", align_bytes=64)
+        w2_codes = keep.tile([P, 2, N], U32, name="w2_codes", align_bytes=64)
+        w2_scales = keep.tile([P, 2, N], U8, name="w2_scales", align_bytes=64)
+        h_codes = keep.tile([P, 2, S], U32, name="h_codes", align_bytes=64)
+        h_scales = keep.tile([P, 2, S], U8, name="h_scales", align_bytes=64)
 
         def cast(grouped, raw, share):
             n = grouped.shape[1]
-            cut = int(n * share) // 4 * 4
+            cut = round(n * share / 4) * 4
             if cut > 0:
                 nc.vector.tensor_copy(out=grouped[:, 0:cut], in_=raw[:, 0:cut])
             if cut < n:
@@ -76,28 +84,25 @@ def tile_picked_place_mlp_gelu_srt_l_kernel(tc, xT, w1, w2, gate, offs, out):
         def quantize(codes, scales, grouped):
             nc.vector.quantize_mx(out=codes.bitcast(FP8X4), scales=scales, in_=grouped)
 
-        x_codes = keep.tile([P, S], U32, name="x_codes", align_bytes=64)
-        x_scales = keep.tile([P, S], U8, name="x_scales", align_bytes=64)
-        w1_codes = keep.tile([P, 2, HALF], U32, name="w1_codes", align_bytes=64)
-        w1_scales = keep.tile([P, 2, HALF], U8, name="w1_scales", align_bytes=64)
-        w2_codes = keep.tile([P, 2, N], U32, name="w2_codes", align_bytes=64)
-        w2_scales = keep.tile([P, 2, N], U8, name="w2_scales", align_bytes=64)
-        h_codes = keep.tile([P, 2, S], U32, name="h_codes", align_bytes=64)
-        h_scales = keep.tile([P, 2, S], U8, name="h_scales", align_bytes=64)
-
-        def do_x(i, share):
-            a, b = x_edges[i]
-            n = b - a
-            g = keep.tile([P, 4 * n], BF16, name=f"x_grouped{i}", align_bytes=64)
+        def plain_operand(name, raw, width, codes, scales, share):
+            g = keep.tile([P, 4 * width], BF16, name=name, align_bytes=64)
             cast(
                 g[:].rearrange("p (c i t) -> p c t i", i=4, t=4),
-                x_raw[i][:].rearrange("p t (c i) -> p c t i", i=4),
+                raw[:].rearrange("p t (c i) -> p c t i", i=4),
                 share,
             )
-            quantize(x_codes[:, a:b], x_scales[:, a:b], g[:])
+            quantize(codes, scales, g[:])
+
+        def do_x(i, share):
+            a, b = tokens[i]
+            plain_operand(f"x_grouped{i}", x_raw[i], b - a, x_codes[:, a:b], x_scales[:, a:b], share)
+
+        def do_w2(c, mh, share):
+            cols = slice(256 * mh, 256 * (mh + 1))
+            plain_operand(f"w2_grouped{c}{mh}", w2_raw[c, mh], 256, w2_codes[:, c, cols], w2_scales[:, c, cols], share)
 
         def do_w1(c, share):
-            g = keep.tile([P, 4 * HALF], BF16, name=f"w1_grouped{c}", align_bytes=64)
+            g = keep.tile([P, 4 * 512], BF16, name=f"w1_grouped{c}", align_bytes=64)
             cast(
                 g[:].rearrange("p (t m j) -> p m j t", t=4, j=4),
                 w1_raw[c][:].rearrange("p j (m t) -> p m j t", t=4),
@@ -105,85 +110,117 @@ def tile_picked_place_mlp_gelu_srt_l_kernel(tc, xT, w1, w2, gate, offs, out):
             )
             quantize(w1_codes[:, c, :], w1_scales[:, c, :], g[:])
 
-        def do_w2(c, share):
-            g = keep.tile([P, 4 * N], BF16, name=f"w2_grouped{c}", align_bytes=64)
-            cast(
-                g[:].rearrange("p (c i t) -> p c t i", i=4, t=4),
-                w2_raw[c][:].rearrange("p t (c i) -> p c t i", i=4),
-                share,
-            )
-            quantize(w2_codes[:, c, :], w2_scales[:, c, :], g[:])
-
         h_grouped = {}
         for c in range(2):
-            for half in range(2):
-                h_grouped[c, half] = keep.tile([P, HALF, 4], BF16, name=f"h_grouped{c}{half}", align_bytes=64)
+            for i in range(3):
+                a, b = tokens[i]
+                h_grouped[c, i] = keep.tile([P, b - a, 4], BF16, name=f"h_grouped{c}{i}", align_bytes=64)
 
-        def layer1(c, b):
-            bank = psum_h.tile([P, 4, BLK], F32, name="bank")
-            cols = slice(b * BLK, (b + 1) * BLK)
-            for t in range(4):
-                nc.tensor.matmul_mx(
-                    out=bank[:, t, :],
-                    lhsT=w1_codes[:, c, t * P : (t + 1) * P].bitcast(FP8X4),
-                    lhsT_scale=w1_scales[:, c, t * P : (t + 1) * P],
-                    rhs=x_codes[:, cols].bitcast(FP8X4),
-                    rhs_scale=x_scales[:, cols],
-                    start=True,
-                    stop=True,
+        def layer1(c, i):
+            a, b = tokens[i]
+            for n0 in range(a, b, 128):
+                bank = psum_h.tile([P, 4, 128], F32, name="bank")
+                cols = slice(n0, n0 + 128)
+                for t in range(4):
+                    nc.tensor.matmul_mx(
+                        out=bank[:, t, :],
+                        lhsT=w1_codes[:, c, t * P : (t + 1) * P].bitcast(FP8X4),
+                        lhsT_scale=w1_scales[:, c, t * P : (t + 1) * P],
+                        rhs=x_codes[:, cols].bitcast(FP8X4),
+                        rhs_scale=x_scales[:, cols],
+                        start=True,
+                        stop=True,
+                    )
+                nc.scalar.activation(
+                    h_grouped[c, i][:, n0 - a : n0 - a + 128, :], bank[:].rearrange("p t n -> p n t"), GELU
                 )
-            half, q = divmod(b, 4)
-            nc.scalar.activation(
-                h_grouped[c, half][:, q * BLK : (q + 1) * BLK, :],
-                bank[:].rearrange("p t n -> p n t"),
-                GELU,
-            )
 
-        def quant_h(c, half):
-            cols = slice(half * HALF, (half + 1) * HALF)
-            quantize(h_codes[:, c, cols], h_scales[:, c, cols], h_grouped[c, half][:].rearrange("p n t -> p (n t)"))
+        def quant_h(c, i):
+            a, b = tokens[i]
+            quantize(h_codes[:, c, a:b], h_scales[:, c, a:b], h_grouped[c, i][:].rearrange("p n t -> p (n t)"))
 
-        def layer2(half, m):
-            bank = psum_y.tile([P, HALF], F32, name="ybank")
-            cols = slice(half * HALF, (half + 1) * HALF)
-            for c in range(2):
-                nc.tensor.matmul_mx(
-                    out=bank[:],
-                    lhsT=w2_codes[:, c, m * P : (m + 1) * P].bitcast(FP8X4),
-                    lhsT_scale=w2_scales[:, c, m * P : (m + 1) * P],
-                    rhs=h_codes[:, c, cols].bitcast(FP8X4),
-                    rhs_scale=h_scales[:, c, cols],
-                    start=(c == 0),
-                    stop=(c == 1),
-                )
-            y = keep.tile([P, HALF], F32, name=f"y{half}{m}")
+        y_sb = {}
+
+        def layer2(i, ms):
+            a, b = tokens[i]
+            n = b - a
+            bank = psum_y.tile([P, 512], F32, name="ybank")
+            y = keep.tile([P, 512], F32, name=f"y{i}{ms[0]}")
+            for k, m in enumerate(ms):
+                for c in range(2):
+                    nc.tensor.matmul_mx(
+                        out=bank[:, k * n : (k + 1) * n],
+                        lhsT=w2_codes[:, c, m * P : (m + 1) * P].bitcast(FP8X4),
+                        lhsT_scale=w2_scales[:, c, m * P : (m + 1) * P],
+                        rhs=h_codes[:, c, a:b].bitcast(FP8X4),
+                        rhs_scale=h_scales[:, c, a:b],
+                        start=(c == 0),
+                        stop=(c == 1),
+                    )
+                y_sb[i, m] = y[:, k * n : (k + 1) * n]
             nc.scalar.copy(out=y[:], in_=bank[:])
-            nc.vector.tensor_tensor(
-                windows[m][:].indirect(offsets[:, half * 32 : (half + 1) * 32]), y[:], gate_sb[:, cols], MULT
-            )
-            if half == 1:
-                nc.sync.dma_start(out=out[m * P : (m + 1) * P, :], in_=windows[m][:])
 
-        do_x(0, 1.0)
+        def scatter(i, m, lo=0, hi=None):
+            a, b = tokens[i]
+            hi = b - a if hi is None else hi
+            nc.vector.tensor_tensor(
+                windows[m][:].indirect(offsets[:, (a + lo) // 16 : (a + hi) // 16]),
+                y_sb[i, m][:, lo:hi],
+                gate_sb[:, a + lo : a + hi],
+                MULT,
+            )
+
+        def store(m, lo, hi):
+            nc.sync.dma_start(out=out[m * P : (m + 1) * P, lo:hi], in_=windows[m][:, lo:hi])
+
+        do_x(0, 0.5)
+        nc.vector.memset(windows[2][:], 0.0)
         do_w1(0, 0.6)
-        do_x(1, 1.0)
-        for b in range(0, 4):
-            layer1(0, b)
-        do_w1(1, 0.6)
+        nc.vector.memset(windows[3][:], 0.0)
+        layer1(0, 0)
+        do_w1(1, 0.75)
         quant_h(0, 0)
-        for b in range(0, 4):
-            layer1(1, b)
-        do_x(2, 1.0)
-        for b in range(4, 8):
-            layer1(0, b)
+        do_w2(0, 0, 0.5)
+        layer1(1, 0)
+        do_w2(1, 0, 0.8)
+        do_x(1, 0)
         quant_h(1, 0)
-        do_w2(0, 1.0)
-        for b in range(4, 8):
-            layer1(1, b)
-        do_w2(1, 1.0)
+        layer2(0, (0, 1))
+        layer1(0, 1)
+        layer1(1, 1)
+        do_x(2, 0.6)
         quant_h(0, 1)
         quant_h(1, 1)
-        for m in range(4):
-            layer2(0, m)
-        for m in range(4):
-            layer2(1, m)
+        scatter(0, 0)
+        scatter(0, 1)
+        layer2(1, (0, 1))
+        layer1(0, 2)
+        do_w2(0, 1, 0.3)
+        do_w2(1, 1, 0.3)
+        scatter(1, 0)
+        scatter(1, 1)
+        store(0, 0, 512)
+        store(1, 0, 512)
+        layer2(0, (2, 3))
+        layer2(1, (2, 3))
+        quant_h(0, 2)
+        layer1(1, 2)
+        scatter(0, 2)
+        scatter(0, 3)
+        scatter(1, 2)
+        scatter(1, 3)
+        store(2, 0, 512)
+        store(3, 0, 512)
+        quant_h(1, 2)
+        for m in (0, 3, 1, 2):
+            layer2(2, (m,))
+        scatter(2, 0)
+        store(0, 512, T)
+        scatter(2, 3, 0, 256)
+        store(3, 512, 768)
+        scatter(2, 1)
+        store(1, 512, T)
+        scatter(2, 2)
+        store(2, 512, T)
+        scatter(2, 3, 256, 512)
+        store(3, 768, T)

@@ -26,50 +26,66 @@ def tile_picked_place_mlp_gelu_srt_l_kernel(tc, xT, w1, w2, gate, offs, out):
         psum_y = ctx.enter_context(tc.psum_pool(name="psum_y", bufs=4))
 
         offsets = keep.tile([P, S // 16], U16, name="offsets")
-        gate_sb = keep.tile([P, S], F32, name="gate_sb")
         warm = keep.tile([P, 8], F32, name="warm")
         nc.vector.memset(warm[:], 0.0)
         nc.scalar.activation(warm[:], warm[:], GELU)
 
-        x_rows = xT.rearrange("(p j) s -> p j s", j=4)
-        w1_rows = w1.rearrange("(p j) h -> p j h", j=4)
+        x_raw, w1_raw, w2_raw, gates, windows, y_sb = {}, {}, {}, {}, {}, {}
 
-        def load(name, src, width):
-            raw = keep.tile([P, 4, width], F32, name=name)
-            nc.sync.dma_start(out=raw[:], in_=src)
+        def load(name, src):
+            raw = keep.tile([P, 4, src.shape[1]], F32, name=name)
+            nc.sync.dma_start(out=raw[:], in_=src.rearrange("(p j) n -> p j n", j=4))
             return raw
 
-        def load_w2(c, mh):
-            rows = w2[512 * c : 512 * (c + 1), 256 * mh : 256 * (mh + 1)].rearrange("(p j) m -> p j m", j=4)
-            return load(f"w2_raw{c}{mh}", rows, 256)
+        def load_x(i, n):
+            raw = load(f"x_raw{i}", xT[:, 256 * i : 256 * (i + n)])
+            for k in range(n):
+                x_raw[i + k] = (raw, 256 * k)
 
-        tokens = [(0, 256), (256, 512), (512, 1024)]
-        x_raw, w1_raw, w2_raw = {}, {}, {}
-        x_raw[0] = load("x_raw0", x_rows[:, :, 0:256], 256)
-        w1_raw[0] = load("w1_raw0", w1_rows[:, :, 0:512], 512)
-        w1_raw[1] = load("w1_raw1", w1_rows[:, :, 512:1024], 512)
-        w2_raw[0, 0] = load_w2(0, 0)
-        w2_raw[1, 0] = load_w2(1, 0)
-        x_raw[1] = load("x_raw1", x_rows[:, :, 256:512], 256)
-        nc.sync.dma_start(offsets[:], offs)
-        nc.sync.dma_start(out=gate_sb[:], in_=gate[0:P, :])
-        x_raw[2] = load("x_raw2", x_rows[:, :, 512:1024], 512)
-        w2_raw[0, 1] = load_w2(0, 1)
-        w2_raw[1, 1] = load_w2(1, 1)
+        def load_w1(c, q, n):
+            first = 512 * c + 256 * q
+            raw = load(f"w1_raw{c}{q}", w1[:, first : first + 256 * n])
+            for k in range(n):
+                w1_raw[c, q + k] = (raw, 256 * k)
 
-        windows = []
+        def load_w2(c):
+            raw = load(f"w2_raw{c}", w2[512 * c : 512 * (c + 1), :])
+            for k in range(2):
+                w2_raw[c, k] = (raw, 256 * k)
+
+        def load_gate():
+            nc.sync.dma_start(offsets[:], offs)
+            g = keep.tile([P, S], F32, name="gate_sb")
+            nc.sync.dma_start(out=g[:], in_=gate[0:P, :])
+            for half in range(2):
+                gates[half] = g[:, 512 * half : 512 * (half + 1)]
+
+        load_w1(0, 0, 2)
+        load_x(0, 2)
+        load_w1(1, 0, 2)
+        load_x(2, 2)
+        load_w2(0)
+        load_w2(1)
+        load_gate()
+
         for m in range(4):
             window = keep.tile([P, T], F32, name=f"window{m}")
-            windows.append(window)
+            windows[m] = window
         nc.vector.memset(windows[0][:], 0.0)
         nc.vector.memset(windows[1][:], 0.0)
+        nc.gpsimd.memset(windows[2][:], 0.0)
+        nc.scalar.copy(out=windows[3][:], in_=windows[0][:])
 
+        x_grouped = keep.tile([P, S, 4], BF16, name="x_grouped", align_bytes=64)
         x_codes = keep.tile([P, S], U32, name="x_codes", align_bytes=64)
         x_scales = keep.tile([P, S], U8, name="x_scales", align_bytes=64)
+        w1_grouped = keep.tile([P, 2, 2048], BF16, name="w1_grouped", align_bytes=64)
         w1_codes = keep.tile([P, 2, 512], U32, name="w1_codes", align_bytes=64)
         w1_scales = keep.tile([P, 2, 512], U8, name="w1_scales", align_bytes=64)
+        w2_grouped = keep.tile([P, 2, N, 4], BF16, name="w2_grouped", align_bytes=64)
         w2_codes = keep.tile([P, 2, N], U32, name="w2_codes", align_bytes=64)
         w2_scales = keep.tile([P, 2, N], U8, name="w2_scales", align_bytes=64)
+        h_grouped = {}
         h_codes = keep.tile([P, 2, S], U32, name="h_codes", align_bytes=64)
         h_scales = keep.tile([P, 2, S], U8, name="h_scales", align_bytes=64)
 
@@ -84,43 +100,48 @@ def tile_picked_place_mlp_gelu_srt_l_kernel(tc, xT, w1, w2, gate, offs, out):
         def quantize(codes, scales, grouped):
             nc.vector.quantize_mx(out=codes.bitcast(FP8X4), scales=scales, in_=grouped)
 
-        def plain_operand(name, raw, width, codes, scales, share):
-            g = keep.tile([P, 4 * width], BF16, name=name, align_bytes=64)
+        def columns(raw_and_first, n):
+            raw, first = raw_and_first
+            return raw[:, :, first : first + 256 * n]
+
+        def cast_plain(grouped, raw, share):
             cast(
-                g[:].rearrange("p (c i t) -> p c t i", i=4, t=4),
-                raw[:].rearrange("p t (c i) -> p c t i", i=4),
+                grouped.rearrange("p (c i) t -> p c t i", i=4),
+                raw.rearrange("p t (c i) -> p c t i", i=4),
                 share,
             )
-            quantize(codes, scales, g[:])
 
-        def do_x(i, share):
-            a, b = tokens[i]
-            plain_operand(f"x_grouped{i}", x_raw[i], b - a, x_codes[:, a:b], x_scales[:, a:b], share)
+        def cast_x(i, n, share):
+            cast_plain(x_grouped[:, 256 * i : 256 * (i + n), :], columns(x_raw[i], n), share)
 
-        def do_w2(c, mh, share):
-            cols = slice(256 * mh, 256 * (mh + 1))
-            plain_operand(f"w2_grouped{c}{mh}", w2_raw[c, mh], 256, w2_codes[:, c, cols], w2_scales[:, c, cols], share)
+        def quant_x(i, n):
+            cols = slice(256 * i, 256 * (i + n))
+            quantize(x_codes[:, cols], x_scales[:, cols], x_grouped[:, cols, :].rearrange("p n t -> p (n t)"))
 
-        def do_w1(c, share):
-            g = keep.tile([P, 4 * 512], BF16, name=f"w1_grouped{c}", align_bytes=64)
+        def cast_w1(c, q, n, share):
+            grouped = w1_grouped[:, c, :].rearrange("p (t m j) -> p m j t", t=4, j=4)
             cast(
-                g[:].rearrange("p (t m j) -> p m j t", t=4, j=4),
-                w1_raw[c][:].rearrange("p j (m t) -> p m j t", t=4),
+                grouped[:, 64 * q : 64 * (q + n)],
+                columns(w1_raw[c, q], n).rearrange("p j (m t) -> p m j t", t=4),
                 share,
             )
-            quantize(w1_codes[:, c, :], w1_scales[:, c, :], g[:])
 
-        h_grouped = {}
-        for c in range(2):
-            for i in range(3):
-                a, b = tokens[i]
-                h_grouped[c, i] = keep.tile([P, b - a, 4], BF16, name=f"h_grouped{c}{i}", align_bytes=64)
+        def quant_w1(c):
+            quantize(w1_codes[:, c, :], w1_scales[:, c, :], w1_grouped[:, c, :])
+
+        def cast_w2(c, k, n, share):
+            cast_plain(w2_grouped[:, c, 256 * k : 256 * (k + n), :], columns(w2_raw[c, k], n), share)
+
+        def quant_w2(c):
+            quantize(w2_codes[:, c, :], w2_scales[:, c, :], w2_grouped[:, c].rearrange("p m t -> p (m t)"))
 
         def layer1(c, i):
-            a, b = tokens[i]
-            for n0 in range(a, b, 128):
+            h = keep.tile([P, 256, 4], BF16, name=f"h_grouped{c}{i}", tag=f"hg{c}{i}", align_bytes=64)
+            h_grouped[c, i] = h
+            for b in (2 * i, 2 * i + 1):
+                h_cols = slice(128 * (b % 2), 128 * (b % 2 + 1))
                 bank = psum_h.tile([P, 4, 128], F32, name="bank")
-                cols = slice(n0, n0 + 128)
+                cols = slice(128 * b, 128 * (b + 1))
                 for t in range(4):
                     nc.tensor.matmul_mx(
                         out=bank[:, t, :],
@@ -131,96 +152,94 @@ def tile_picked_place_mlp_gelu_srt_l_kernel(tc, xT, w1, w2, gate, offs, out):
                         start=True,
                         stop=True,
                     )
-                nc.scalar.activation(
-                    h_grouped[c, i][:, n0 - a : n0 - a + 128, :], bank[:].rearrange("p t n -> p n t"), GELU
-                )
+                nc.scalar.activation(h[:, h_cols, :], bank[:].rearrange("p t n -> p n t"), GELU)
 
-        def quant_h(c, i):
-            a, b = tokens[i]
-            quantize(h_codes[:, c, a:b], h_scales[:, c, a:b], h_grouped[c, i][:].rearrange("p n t -> p (n t)"))
+        def quant_h(c, i, n=1):
+            cols = slice(256 * i, 256 * (i + 1))
+            quantize(h_codes[:, c, cols], h_scales[:, c, cols], h_grouped[c, i][:].rearrange("p n t -> p (n t)"))
 
-        y_sb = {}
-
-        def layer2(i, ms):
-            a, b = tokens[i]
-            n = b - a
+        def layer2(half, m):
+            cols = slice(512 * half, 512 * (half + 1))
+            m_cols = slice(P * m, P * (m + 1))
             bank = psum_y.tile([P, 512], F32, name="ybank")
-            y = keep.tile([P, 512], F32, name=f"y{i}{ms[0]}")
-            for k, m in enumerate(ms):
-                for c in range(2):
-                    nc.tensor.matmul_mx(
-                        out=bank[:, k * n : (k + 1) * n],
-                        lhsT=w2_codes[:, c, m * P : (m + 1) * P].bitcast(FP8X4),
-                        lhsT_scale=w2_scales[:, c, m * P : (m + 1) * P],
-                        rhs=h_codes[:, c, a:b].bitcast(FP8X4),
-                        rhs_scale=h_scales[:, c, a:b],
-                        start=(c == 0),
-                        stop=(c == 1),
-                    )
-                y_sb[i, m] = y[:, k * n : (k + 1) * n]
+            for c in range(2):
+                nc.tensor.matmul_mx(
+                    out=bank[:],
+                    lhsT=w2_codes[:, c, m_cols].bitcast(FP8X4),
+                    lhsT_scale=w2_scales[:, c, m_cols],
+                    rhs=h_codes[:, c, cols].bitcast(FP8X4),
+                    rhs_scale=h_scales[:, c, cols],
+                    start=(c == 0),
+                    stop=(c == 1),
+                )
+            y = keep.tile([P, 512], F32, name=f"y{half}{m}", tag=f"hg{m // 2}{2 + m % 2}" if half == 0 else f"y1{m}", align_bytes=64)
             nc.scalar.copy(out=y[:], in_=bank[:])
+            y_sb[half, m] = y
 
-        def scatter(i, m, lo=0, hi=None):
-            a, b = tokens[i]
-            hi = b - a if hi is None else hi
+        def scatter(half, m, lo=0, hi=512):
+            first = 512 * half
             nc.vector.tensor_tensor(
-                windows[m][:].indirect(offsets[:, (a + lo) // 16 : (a + hi) // 16]),
-                y_sb[i, m][:, lo:hi],
-                gate_sb[:, a + lo : a + hi],
+                windows[m][:].indirect(offsets[:, (first + lo) // 16 : (first + hi) // 16]),
+                y_sb[half, m][:, lo:hi],
+                gates[half][:, lo:hi],
                 MULT,
             )
 
         def store(m, lo, hi):
             nc.sync.dma_start(out=out[m * P : (m + 1) * P, lo:hi], in_=windows[m][:, lo:hi])
 
-        do_x(0, 0.5)
-        nc.vector.memset(windows[2][:], 0.0)
-        do_w1(0, 0.6)
-        nc.vector.memset(windows[3][:], 0.0)
+        cast_w1(0, 0, 2, 0.55)
+        cast_x(0, 1, 0.6)
+        quant_w1(0)
+        cast_x(1, 1, 0.5)
+        quant_x(0, 1)
         layer1(0, 0)
-        do_w1(1, 0.75)
-        quant_h(0, 0)
-        do_w2(0, 0, 0.5)
-        layer1(1, 0)
-        do_w2(1, 0, 0.8)
-        do_x(1, 0)
-        quant_h(1, 0)
-        layer2(0, (0, 1))
+        quant_x(1, 1)
         layer1(0, 1)
-        layer1(1, 1)
-        do_x(2, 0.6)
+        cast_w1(1, 0, 2, 1)
+        quant_h(0, 0)
+        quant_w1(1)
+        layer1(1, 0)
+        cast_x(2, 1, 1)
+        cast_x(3, 1, 1)
         quant_h(0, 1)
-        quant_h(1, 1)
-        scatter(0, 0)
-        scatter(0, 1)
-        layer2(1, (0, 1))
+        layer1(1, 1)
+        quant_x(2, 2)
         layer1(0, 2)
-        do_w2(0, 1, 0.3)
-        do_w2(1, 1, 0.3)
-        scatter(1, 0)
-        scatter(1, 1)
-        store(0, 0, 512)
-        store(1, 0, 512)
-        layer2(0, (2, 3))
-        layer2(1, (2, 3))
-        quant_h(0, 2)
+        cast_w2(0, 0, 2, 1)
+        quant_h(1, 0)
+        quant_w2(0)
+        layer1(0, 3)
+        cast_w2(1, 0, 2, 1)
+        quant_h(1, 1)
+        quant_w2(1)
         layer1(1, 2)
-        scatter(0, 2)
-        scatter(0, 3)
-        scatter(1, 2)
-        scatter(1, 3)
-        store(2, 0, 512)
-        store(3, 0, 512)
+        quant_h(0, 2)
+        layer1(1, 3)
+        quant_h(0, 3)
         quant_h(1, 2)
-        for m in (0, 3, 1, 2):
-            layer2(2, (m,))
-        scatter(2, 0)
+        quant_h(1, 3)
+        layer2(0, 0)
+        layer2(0, 1)
+        layer2(0, 2)
+        layer2(0, 3)
+        scatter(0, 0)
+        store(0, 0, 512)
+        scatter(0, 1)
+        store(1, 0, 512)
+        scatter(0, 2)
+        store(2, 0, 512)
+        layer2(1, 0)
+        layer2(1, 1)
+        layer2(1, 2)
+        layer2(1, 3)
+        scatter(1, 0)
         store(0, 512, T)
-        scatter(2, 3, 0, 256)
-        store(3, 512, 768)
-        scatter(2, 1)
+        scatter(0, 3)
+        store(3, 0, 512)
+        scatter(1, 1)
         store(1, 512, T)
-        scatter(2, 2)
+        scatter(1, 2)
         store(2, 512, T)
-        scatter(2, 3, 256, 512)
-        store(3, 768, T)
+        scatter(1, 3)
+        store(3, 512, T)

from contextlib import ExitStack

import concourse.mybir as mybir

K, T, S, H, N = 512, 2048, 1024, 1024, 512
FLOPS = 2 * S * (K * H + H * N)
BYTES = 4 * (K * S + K * H + H * N + S + N * T) + 2 * 128 * S // 16

F32 = mybir.dt.float32
BF16 = mybir.dt.bfloat16
U32 = mybir.dt.uint32
U16 = mybir.dt.uint16
U8 = mybir.dt.uint8
FP8X4 = mybir.dt.float8_e4m3fn_x4
GELU = mybir.ActivationFunctionType.Gelu_apprx_tanh
MULT = mybir.AluOpType.mult

P = 128


def tile_picked_place_mlp_gelu_srt_l_kernel(tc, xT, w1, w2, gate, offs, out):
    nc = tc.nc
    with ExitStack() as ctx:
        keep = ctx.enter_context(tc.tile_pool(name="keep", bufs=1))
        psum_h = ctx.enter_context(tc.psum_pool(name="psum_h", bufs=4))
        psum_y = ctx.enter_context(tc.psum_pool(name="psum_y", bufs=4))

        offsets = keep.tile([P, S // 16], U16, name="offsets")
        warm = keep.tile([P, 8], F32, name="warm")
        nc.vector.memset(warm[:], 0.0)
        nc.scalar.activation(warm[:], warm[:], GELU)

        x_raw, w1_raw, w2_raw, gates, windows, y_sb = {}, {}, {}, {}, {}, {}

        def load(name, src):
            raw = keep.tile([P, 4, src.shape[1]], F32, name=name)
            nc.sync.dma_start(out=raw[:], in_=src.rearrange("(p j) n -> p j n", j=4))
            return raw

        def load_x(i, n):
            raw = load(f"x_raw{i}", xT[:, 256 * i : 256 * (i + n)])
            for k in range(n):
                x_raw[i + k] = (raw, 256 * k)

        def load_w1(c, q, n):
            first = 512 * c + 256 * q
            raw = load(f"w1_raw{c}{q}", w1[:, first : first + 256 * n])
            for k in range(n):
                w1_raw[c, q + k] = (raw, 256 * k)

        def load_w2(c):
            raw = load(f"w2_raw{c}", w2[512 * c : 512 * (c + 1), :])
            for k in range(2):
                w2_raw[c, k] = (raw, 256 * k)

        def load_gate():
            nc.sync.dma_start(offsets[:], offs)
            g = keep.tile([P, S], F32, name="gate_sb")
            nc.sync.dma_start(out=g[:], in_=gate[0:P, :])
            for half in range(2):
                gates[half] = g[:, 512 * half : 512 * (half + 1)]

        load_w1(0, 0, 2)
        load_x(0, 2)
        load_w1(1, 0, 2)
        load_x(2, 2)
        load_w2(0)
        load_w2(1)
        load_gate()

        for m in range(4):
            window = keep.tile([P, T], F32, name=f"window{m}")
            windows[m] = window
        nc.vector.memset(windows[0][:], 0.0)
        nc.vector.memset(windows[1][:], 0.0)
        nc.gpsimd.memset(windows[2][:], 0.0)
        nc.scalar.copy(out=windows[3][:], in_=windows[0][:])

        x_grouped = keep.tile([P, S, 4], BF16, name="x_grouped", align_bytes=64)
        x_codes = keep.tile([P, S], U32, name="x_codes", align_bytes=64)
        x_scales = keep.tile([P, S], U8, name="x_scales", align_bytes=64)
        w1_grouped = keep.tile([P, 2, 2048], BF16, name="w1_grouped", align_bytes=64)
        w1_codes = keep.tile([P, 2, 512], U32, name="w1_codes", align_bytes=64)
        w1_scales = keep.tile([P, 2, 512], U8, name="w1_scales", align_bytes=64)
        w2_grouped = keep.tile([P, 2, N, 4], BF16, name="w2_grouped", align_bytes=64)
        w2_codes = keep.tile([P, 2, N], U32, name="w2_codes", align_bytes=64)
        w2_scales = keep.tile([P, 2, N], U8, name="w2_scales", align_bytes=64)
        h_grouped = {}
        h_codes = keep.tile([P, 2, S], U32, name="h_codes", align_bytes=64)
        h_scales = keep.tile([P, 2, S], U8, name="h_scales", align_bytes=64)

        def cast(grouped, raw, share):
            n = grouped.shape[1]
            cut = round(n * share / 4) * 4
            if cut > 0:
                nc.vector.tensor_copy(out=grouped[:, 0:cut], in_=raw[:, 0:cut])
            if cut < n:
                nc.scalar.copy(out=grouped[:, cut:n], in_=raw[:, cut:n])

        def quantize(codes, scales, grouped):
            nc.vector.quantize_mx(out=codes.bitcast(FP8X4), scales=scales, in_=grouped)

        def columns(raw_and_first, n):
            raw, first = raw_and_first
            return raw[:, :, first : first + 256 * n]

        def cast_plain(grouped, raw, share):
            cast(
                grouped.rearrange("p (c i) t -> p c t i", i=4),
                raw.rearrange("p t (c i) -> p c t i", i=4),
                share,
            )

        def cast_x(i, n, share):
            cast_plain(x_grouped[:, 256 * i : 256 * (i + n), :], columns(x_raw[i], n), share)

        def quant_x(i, n):
            cols = slice(256 * i, 256 * (i + n))
            quantize(x_codes[:, cols], x_scales[:, cols], x_grouped[:, cols, :].rearrange("p n t -> p (n t)"))

        def cast_w1(c, q, n, share):
            grouped = w1_grouped[:, c, :].rearrange("p (t m j) -> p m j t", t=4, j=4)
            cast(
                grouped[:, 64 * q : 64 * (q + n)],
                columns(w1_raw[c, q], n).rearrange("p j (m t) -> p m j t", t=4),
                share,
            )

        def quant_w1(c):
            quantize(w1_codes[:, c, :], w1_scales[:, c, :], w1_grouped[:, c, :])

        def cast_w2(c, k, n, share):
            cast_plain(w2_grouped[:, c, 256 * k : 256 * (k + n), :], columns(w2_raw[c, k], n), share)

        def quant_w2(c):
            quantize(w2_codes[:, c, :], w2_scales[:, c, :], w2_grouped[:, c].rearrange("p m t -> p (m t)"))

        def layer1(c, i):
            h = keep.tile([P, 256, 4], BF16, name=f"h_grouped{c}{i}", tag=f"hg{c}{i}", align_bytes=64)
            h_grouped[c, i] = h
            for b in (2 * i, 2 * i + 1):
                h_cols = slice(128 * (b % 2), 128 * (b % 2 + 1))
                bank = psum_h.tile([P, 4, 128], F32, name="bank")
                cols = slice(128 * b, 128 * (b + 1))
                for t in range(4):
                    nc.tensor.matmul_mx(
                        out=bank[:, t, :],
                        lhsT=w1_codes[:, c, t * P : (t + 1) * P].bitcast(FP8X4),
                        lhsT_scale=w1_scales[:, c, t * P : (t + 1) * P],
                        rhs=x_codes[:, cols].bitcast(FP8X4),
                        rhs_scale=x_scales[:, cols],
                        start=True,
                        stop=True,
                    )
                nc.scalar.activation(h[:, h_cols, :], bank[:].rearrange("p t n -> p n t"), GELU)

        def quant_h(c, i, n=1):
            cols = slice(256 * i, 256 * (i + 1))
            quantize(h_codes[:, c, cols], h_scales[:, c, cols], h_grouped[c, i][:].rearrange("p n t -> p (n t)"))

        def layer2(half, m):
            cols = slice(512 * half, 512 * (half + 1))
            m_cols = slice(P * m, P * (m + 1))
            bank = psum_y.tile([P, 512], F32, name="ybank")
            for c in range(2):
                nc.tensor.matmul_mx(
                    out=bank[:],
                    lhsT=w2_codes[:, c, m_cols].bitcast(FP8X4),
                    lhsT_scale=w2_scales[:, c, m_cols],
                    rhs=h_codes[:, c, cols].bitcast(FP8X4),
                    rhs_scale=h_scales[:, c, cols],
                    start=(c == 0),
                    stop=(c == 1),
                )
            y = keep.tile([P, 512], F32, name=f"y{half}{m}", tag=f"hg{m // 2}{2 + m % 2}" if half == 0 else f"y1{m}", align_bytes=64)
            nc.scalar.copy(out=y[:], in_=bank[:])
            y_sb[half, m] = y

        def scatter(half, m, lo=0, hi=512):
            first = 512 * half
            nc.vector.tensor_tensor(
                windows[m][:].indirect(offsets[:, (first + lo) // 16 : (first + hi) // 16]),
                y_sb[half, m][:, lo:hi],
                gates[half][:, lo:hi],
                MULT,
            )

        def store(m, lo, hi):
            nc.sync.dma_start(out=out[m * P : (m + 1) * P, lo:hi], in_=windows[m][:, lo:hi])

        cast_w1(0, 0, 2, 0.55)
        cast_x(0, 1, 0.6)
        quant_w1(0)
        cast_x(1, 1, 0.5)
        quant_x(0, 1)
        layer1(0, 0)
        quant_x(1, 1)
        layer1(0, 1)
        cast_w1(1, 0, 2, 1)
        quant_h(0, 0)
        quant_w1(1)
        layer1(1, 0)
        cast_x(2, 1, 1)
        cast_x(3, 1, 1)
        quant_h(0, 1)
        layer1(1, 1)
        quant_x(2, 2)
        layer1(0, 2)
        cast_w2(0, 0, 2, 1)
        quant_h(1, 0)
        quant_w2(0)
        layer1(0, 3)
        cast_w2(1, 0, 2, 1)
        quant_h(1, 1)
        quant_w2(1)
        layer1(1, 2)
        quant_h(0, 2)
        layer1(1, 3)
        quant_h(0, 3)
        quant_h(1, 2)
        quant_h(1, 3)
        layer2(0, 0)
        layer2(0, 1)
        layer2(0, 2)
        layer2(0, 3)
        scatter(0, 0)
        store(0, 0, 512)
        scatter(0, 1)
        store(1, 0, 512)
        scatter(0, 2)
        store(2, 0, 512)
        layer2(1, 0)
        layer2(1, 1)
        layer2(1, 2)
        layer2(1, 3)
        scatter(1, 0)
        store(0, 512, T)
        scatter(0, 3)
        store(3, 0, 512)
        scatter(1, 1)
        store(1, 512, T)
        scatter(1, 2)
        store(2, 512, T)
        scatter(1, 3)
        store(3, 512, T)
